import numpy as np
import ml_dtypes


def mxq(x, axis, fmt="e4m3"):
    dtype, down = {"e4m3": (ml_dtypes.float8_e4m3fn, 7), "e5m2": (ml_dtypes.float8_e5m2, 14)}[fmt]
    v = np.moveaxis(np.asarray(x, np.float32).astype(ml_dtypes.bfloat16).astype(np.float64), axis, -1)
    blocks = v.reshape(v.shape[:-1] + (-1, 32))
    amax = np.abs(blocks).max(-1, keepdims=True)
    byte = np.maximum(np.where(amax > 0, np.frexp(amax)[1] - 1 + 127, 0) - down, 1)
    scale = np.exp2(byte - 127.0)
    codes = (blocks / scale).astype(np.float32).astype(dtype).astype(np.float64)
    return np.moveaxis((codes * scale).reshape(v.shape), -1, axis)


WIDE = False


def mx_kscale(k):
    if not WIDE:
        return np.ones(k)
    levels = np.array([10, -10, 5, -5, 0])
    if k % 512:
        return np.exp2(np.random.permutation(np.resize(levels, k // 32))).repeat(32)
    a = np.empty((k // 512, 16))
    for p in range(k // 512):
        a[p, :8] = np.random.permutation(np.resize(levels, 8))
        for g in range(8):
            far = levels[np.abs(levels - a[p, g]) >= 10]
            a[p, g + 8] = far[np.random.randint(len(far))]
    return np.exp2(a.ravel()).repeat(32)


def f64(x):
    return np.asarray(x).astype(np.float64)


def striped(idx):
    return np.tile(np.asarray(idx).reshape(-1, 16).T, (8, 1)).astype(np.uint16)


def unstriped(offs):
    return offs[:16].T.reshape(-1).astype(np.int64)


E2M1 = np.array([0.0, 0.5, 1.0, 1.5, 2.0, 3.0, 4.0, 6.0, -0.0, -0.5, -1.0, -1.5, -2.0, -3.0, -4.0, -6.0])


def pack_weight(w, fmt):
    k, n = w.shape
    w = f64(np.asarray(w, np.float32).astype(ml_dtypes.bfloat16)).reshape(k // 32, 32, n)
    amax = np.abs(w).max(1)
    if fmt == "e4m3":
        byte = np.frexp(amax)[1] - 1 + 127 - 7
    else:
        mant, ex = np.frexp(amax / 6.0)
        byte = np.where(mant > 0.5, ex, ex - 1) + 127
    byte = np.clip(np.where(amax > 0, byte, 1), 1, 254)
    scaled = (w * np.exp2(127.0 - byte)[:, None, :]).reshape(k, n).astype(np.float32)
    by_word = np.ascontiguousarray(scaled.reshape(k // 512, 128, 4, n).transpose(0, 1, 3, 2))
    if fmt == "e4m3":
        words = by_word.astype(ml_dtypes.float8_e4m3fn).view(np.uint8)
    else:
        c = by_word.astype(ml_dtypes.float4_e2m1fn).view(np.uint8) & 0xF
        words = (c[..., 0::2] | (c[..., 1::2] << 4)).reshape(k // 512, 128, 2 * n)
    return np.ascontiguousarray(words), np.ascontiguousarray(byte.astype(np.uint8).reshape(k // 512, 16, n))


def unpack_weight(words, scales, fmt):
    g, _, n = scales.shape
    words = np.ascontiguousarray(words).reshape(g, 128, n, -1)
    if fmt == "e4m3":
        vals = words.view(ml_dtypes.float8_e4m3fn).astype(np.float64)
    else:
        nib = np.empty((g, 128, n, 4), np.uint8)
        nib[..., 0::2] = words & 0xF
        nib[..., 1::2] = words >> 4
        vals = E2M1[nib]
    vals = vals * np.repeat(np.exp2(scales.astype(np.float64) - 127.0), 8, axis=1)[..., None]
    return vals.transpose(0, 1, 3, 2).reshape(g * 512, n)


D, E, T, I, Q, G = 512, 512, 1024, 256, 512, 32


def setup_inputs():
    n = np.random.standard_normal
    idx = np.random.permutation(T)[:I]
    fd = mx_kscale(D)
    fq = mx_kscale(Q)
    keysp = pack_weight(n((D, T)) / fd[:, None], "e4m3")
    return {
        "query": (n((D, Q)) * 0.7 / np.sqrt(D) * fd[:, None]).astype(np.float32),
        "keys_words": keysp[0],
        "keys_scales": keysp[1],
        "share": (np.random.uniform(0.2, 0.8, (Q, 1))).astype(np.float32),
        "qs": (np.random.uniform(2.0, 8.0, (Q, 1)) * fq[:, None]).astype(np.float32),
        "grows": (n((Q, E)) / fq[:, None]).astype(np.float32),
        "old": (n((E, T)) * 2.0).astype(np.float32),
        "fade": (np.random.uniform(0.5, 1.0, (1, T))).astype(np.float32),
        "offs": striped(idx),
    }


def reference(query, keys_words, keys_scales, share, qs, grows, old, fade, offs):
    idx = unstriped(offs)
    keysu = unpack_weight(keys_words, keys_scales, "e4m3")
    queryq = mxq(f64(query), 0, "e4m3")
    keysidxg = keysu[:, idx]
    a = queryq.T @ keysidxg
    p = np.exp(a)
    z = np.sum(p, axis=1, keepdims=True)
    s = p.reshape(Q, G, I // G).sum(axis=2)
    v1 = 1.0 / (z * f64(share) + s * (1.0 - f64(share)) * 64.0)
    vr = np.repeat(v1, I // G, axis=1)
    w = p * vr
    wq = w * f64(qs)
    growsq = mxq(f64(grows), 0, "e4m3")
    wqq = mxq(wq, 0, "e4m3")
    gv = growsq.T @ wqq
    gf = np.zeros((E, T))
    gf[:, idx] = gv
    y = f64(old) * f64(fade) + gf
    return y

@@ -1,0 +1,241 @@
+from contextlib import ExitStack
+
+import concourse.mybir as mybir
+from concourse.masks import make_identity
+
+D, E, T, I, Q, G = 512, 512, 1024, 256, 512, 32
+FLOPS = 2 * D * Q * I + 2 * Q * E * I
+
+F32 = mybir.dt.float32
+BF16 = mybir.dt.bfloat16
+I32 = mybir.dt.int32
+U32 = mybir.dt.uint32
+U16 = mybir.dt.uint16
+U8 = mybir.dt.uint8
+FP8X4 = mybir.dt.float8_e4m3fn_x4
+ALU = mybir.AluOpType
+ACT = mybir.ActivationFunctionType
+AX = mybir.AxisListType
+
+P = 128
+PACK = 4
+BANK = 512
+GROUP = I // G
+
+
+def tile_attend_bmixednorm_v_kernel(tc, query, keys_words, keys_scales, share, qs, grows, old, fade, offs, out):
+    nc = tc.nc
+    with ExitStack() as ctx:
+        sb = ctx.enter_context(tc.tile_pool(name="sb", bufs=1))
+        ps = ctx.enter_context(tc.psum_pool(name="ps", bufs=1))
+
+        def bank(n, name):
+            return ps.tile([P, BANK], F32, name=name, tag="bank%d" % n)
+
+        offsets = sb.tile([P, I // 16], U16, name="offsets")
+        key_bytes = sb.tile([P, T], U8, name="key_bytes", align_bytes=64)
+        nc.gpsimd.memset(key_bytes[:].bitcast(I32), 0)
+        nc.sync.dma_start(offsets[:], offs)
+        query_rows = query.rearrange("(p j) q -> p j q", j=PACK)
+        q_raw = [sb.tile([P, PACK, Q // 2], F32, name="q_raw%d" % h) for h in range(2)]
+        nc.sync.dma_start(out=q_raw[0][:], in_=query_rows[:, :, 0 : Q // 2])
+        for quad in range(4):
+            nc.sync.dma_start(
+                out=key_bytes[32 * quad : 32 * quad + 4, :].bitcast(I32),
+                in_=keys_scales[0, 4 * quad : 4 * quad + 4, :].bitcast(I32),
+            )
+        nc.sync.dma_start(out=q_raw[1][:], in_=query_rows[:, :, Q // 2 : Q])
+        key_words = sb.tile([P, T], U32, name="key_words", align_bytes=64)
+        nc.sync.dma_start(out=key_words[:].bitcast(I32), in_=keys_words[0].rearrange("p n t -> p (n t)").bitcast(I32))
+        share_sb = sb.tile([P, PACK], F32, name="share_sb")
+        nc.sync.dma_start(out=share_sb[:], in_=share.rearrange("(p r) o -> p (r o)", r=PACK))
+        qs_sb = sb.tile([P, PACK], F32, name="qs_sb")
+        nc.sync.dma_start(out=qs_sb[:], in_=qs.rearrange("(p r) o -> p (r o)", r=PACK))
+        fade_rows = sb.tile([P, P], F32, name="fade_rows")
+        nc.vector.memset(fade_rows[:], 0.0)
+        nc.sync.dma_start(out=fade_rows[0 : T // P, :], in_=fade.rearrange("o (b t) -> (o b) t", t=P))
+        g_raw = sb.tile([P, PACK, E], F32, name="g_raw")
+        nc.sync.dma_start(out=g_raw[:], in_=grows.rearrange("(p r) e -> p r e", r=PACK))
+        old_rows = old.rearrange("(m p) t -> p m t", p=P)
+        old_sb = []
+        for h in range(2):
+            t = sb.tile([P, 2, T], F32, name="old%d" % h)
+            nc.sync.dma_start(out=t[:], in_=old_rows[:, 2 * h : 2 * h + 2, :])
+            old_sb.append(t)
+
+        ident = sb.tile([P, P], F32, name="ident")
+        make_identity(nc, ident[:])
+        windows = []
+        for m in range(2):
+            w = sb.tile([P, T], F32, name="window%d" % m)
+            nc.vector.memset(w[:], 0.0)
+            windows.append(w)
+
+        kg_bytes = sb.tile([P, I], U8, name="kg_bytes", align_bytes=64)
+        nc.vector.tensor_copy(kg_bytes[:], key_bytes[:].indirect(offsets[:]))
+
+        q_bf = sb.tile([P, PACK, P, PACK], BF16, name="q_bf", align_bytes=64)
+        for h in range(2):
+            nc.vector.tensor_copy(
+                out=q_bf[:, :, h * (P // 2) : (h + 1) * (P // 2), :].rearrange("p r s j -> p s j r"),
+                in_=q_raw[h][:].rearrange("p j (s r) -> p s j r", r=PACK),
+            )
+        q_words = sb.tile([P, Q], U32, name="q_words", align_bytes=64)
+        q_bytes = sb.tile([P, Q], U8, name="q_bytes", align_bytes=64)
+        neg_max = sb.tile([P, PACK], F32, name="neg_max", tag="neg_max_then_g_bf", align_bytes=64)
+        p_sb = sb.tile([P, PACK, I], F32, name="p_sb")
+        z = sb.tile([P, PACK], F32, name="z")
+        nc.vector.quantize_mx(
+            out=q_words[:].bitcast(FP8X4), scales=q_bytes[:], in_=q_bf[:].rearrange("p r s j -> p (r s j)")
+        )
+        kg_words = sb.tile([P, I], U32, name="kg_words", align_bytes=64)
+        nc.vector.tensor_copy(kg_words[:], key_words[:].indirect(offsets[:]))
+        scores = []
+        for r in range(PACK):
+            cols = slice(r * P, (r + 1) * P)
+            a = bank(r, "scores%d" % r)
+            nc.tensor.matmul_mx(
+                out=a[:, 0:I],
+                lhsT=q_words[:, cols].bitcast(FP8X4),
+                lhsT_scale=q_bytes[:, cols],
+                rhs=kg_words[:].bitcast(FP8X4),
+                rhs_scale=kg_bytes[:],
+                start=True,
+                stop=True,
+            )
+            scores.append(a)
+
+        inv_qs = sb.tile([P, PACK], F32, name="inv_qs")
+        nc.vector.reciprocal(inv_qs[:], qs_sb[:])
+        row_mix = sb.tile([P, PACK], F32, name="row_mix")
+        nc.gpsimd.tensor_tensor(row_mix[:], share_sb[:], inv_qs[:], ALU.mult)
+        rest = sb.tile([P, PACK], F32, name="rest")
+        nc.gpsimd.tensor_scalar(rest[:], share_sb[:], -64.0, 64.0, ALU.mult, ALU.add)
+        group_mix = sb.tile([P, PACK], F32, name="group_mix")
+        nc.gpsimd.tensor_tensor(group_mix[:], rest[:], inv_qs[:], ALU.mult)
+
+        for r in range(PACK):
+            nc.vector.tensor_reduce(neg_max[:, r : r + 1], scores[r][:, 0:I], AX.X, ALU.max, negate=True)
+            nc.scalar.activation(
+                p_sb[:, r, :], scores[r][:, 0:I], ACT.Exp, bias=neg_max[:, r : r + 1], accum_out=z[:, r : r + 1]
+            )
+        s = sb.tile([P, PACK, G], F32, name="s")
+        for r in range(PACK):
+            nc.vector.tensor_reduce(s[:, r, :], p_sb[:, r, :].rearrange("p (g j) -> p g j", j=GROUP), AX.X, ALU.add)
+        z_mix = sb.tile([P, PACK], F32, name="z_mix")
+        nc.vector.tensor_tensor(z_mix[:], z[:], row_mix[:], ALU.mult)
+        den = sb.tile([P, PACK, G], F32, name="den")
+        for r in range(PACK):
+            nc.vector.tensor_scalar(
+                den[:, r, :], s[:, r, :], group_mix[:, r : r + 1], z_mix[:, r : r + 1], ALU.mult, ALU.add
+            )
+
+        g_bf = sb.tile([P, E, PACK], BF16, name="g_bf", tag="neg_max_then_g_bf", align_bytes=64)
+        g_words = sb.tile([P, E], U32, name="g_words", align_bytes=64)
+        g_bytes = sb.tile([P, E], U8, name="g_bytes", align_bytes=64)
+        for m in range(E // P):
+            cols = slice(m * P, (m + 1) * P)
+            nc.scalar.copy(
+                out=g_bf[:, cols, :].rearrange("p (c i) r -> p c r i", i=4),
+                in_=g_raw[:, :, cols].rearrange("p r (c i) -> p c r i", i=4),
+            )
+
+        w_words = sb.tile([P, I], U32, name="w_words", align_bytes=64)
+        w_bytes = sb.tile([P, I], U8, name="w_bytes", align_bytes=64)
+        gv = sb.tile([P, E // P, I], F32, name="gv")
+        for h in range(2):
+            gs = slice(h * (G // 2), (h + 1) * (G // 2))
+            slots = slice(h * P, (h + 1) * P)
+            v = sb.tile([P, G // 2, PACK], F32, name="v%d" % h, tag="stage%d" % h, align_bytes=64)
+            w_bf = sb.tile([P, P, PACK], BF16, name="w_bf%d" % h, tag="stage%d" % (h + 1), align_bytes=64)
+            nc.vector.reciprocal(v[:].rearrange("p g r -> p r g"), den[:, :, gs])
+            if h == 0:
+                for m in range(E // P):
+                    cols = slice(m * P, (m + 1) * P)
+                    nc.vector.quantize_mx(
+                        out=g_words[:, cols].bitcast(FP8X4),
+                        scales=g_bytes[:, cols],
+                        in_=g_bf[:, cols, :].rearrange("p e r -> p (e r)"),
+                    )
+            nc.vector.tensor_tensor(
+                w_bf[:].rearrange("p (g j) r -> p g j r", j=GROUP),
+                p_sb[:, :, slots].rearrange("p r (g j) -> p g j r", j=GROUP),
+                v[:].unsqueeze(2).to_broadcast([P, G // 2, GROUP, PACK]),
+                ALU.mult,
+            )
+            nc.vector.quantize_mx(
+                out=w_words[:, slots].bitcast(FP8X4),
+                scales=w_bytes[:, slots],
+                in_=w_bf[:].rearrange("p i r -> p (i r)"),
+            )
+            first = bank(2 * h, "gv_first%d" % h)
+            others = bank(2 * h + 1, "gv_others%d" % h)
+            for m in range(E // P):
+                cols = slice(m * P, (m + 1) * P)
+                nc.tensor.matmul_mx(
+                    out=first[:, 0:P] if m == 0 else others[:, (m - 1) * P : m * P],
+                    lhsT=g_words[:, cols].bitcast(FP8X4),
+                    lhsT_scale=g_bytes[:, cols],
+                    rhs=w_words[:, slots].bitcast(FP8X4),
+                    rhs_scale=w_bytes[:, slots],
+                    start=True,
+                    stop=True,
+                )
+            nc.scalar.copy(out=gv[:, 0, slots], in_=first[:, 0:P])
+            nc.scalar.copy(out=gv[:, 1:, slots], in_=others[:, 0 : 3 * P].rearrange("p (m i) -> p m i", i=P))
+
+        fade_ps = bank(6, "fade_ps")
+        nc.tensor.transpose(fade_ps[:, 0:P], fade_rows[:], ident[:])
+        fade_cols = sb.tile([P, T // P], F32, name="fade_cols")
+        nc.vector.tensor_copy(fade_cols[:], fade_ps[:, 0 : T // P])
+
+        def fade_turned(pair):
+            y = sb.tile([P, T // P, 2 * P], F32, name="faded_t%d" % pair)
+            for b2 in range(T // P // 2):
+                turned = bank(4 + b2 % 2, "turned%d_%d" % (pair, b2))
+                for k in range(2):
+                    b = 2 * b2 + k
+                    for m in range(2):
+                        nc.tensor.transpose(
+                            turned[:, (2 * k + m) * P : (2 * k + m + 1) * P], old_sb[pair][:, m, b * P : (b + 1) * P], ident[:]
+                        )
+                for k in range(2):
+                    b = 2 * b2 + k
+                    nc.scalar.activation(
+                        y[:, b, :], turned[:, 2 * k * P : (2 * k + 2) * P], ACT.Copy, scale=fade_cols[:, b : b + 1]
+                    )
+            return y
+
+        def turn_back(y, m, banks):
+            backs = []
+            for h in range(2):
+                back = bank(banks[h], "back%d_%d" % (m, h))
+                for k in range(4):
+                    nc.tensor.transpose(back[:, k * P : (k + 1) * P], y[:, 4 * h + k, (m % 2) * P : (m % 2 + 1) * P], ident[:])
+                backs.append(back)
+            return backs
+
+        def scatter(m):
+            nc.vector.tensor_copy(windows[m % 2][:].indirect(offsets[:]), gv[:, m, :])
+
+        def add_and_store(m, backs):
+            res = sb.tile([P, T], F32, name="res%d" % m)
+            for h in range(2):
+                cols = slice(h * BANK, (h + 1) * BANK)
+                nc.vector.tensor_tensor(res[:, cols], backs[h][:], windows[m % 2][:, cols], ALU.add)
+                if m == E // P - 1:
+                    nc.sync.dma_start(out=out[m * P : (m + 1) * P, cols], in_=res[:, cols])
+            if m < E // P - 1:
+                nc.sync.dma_start(out=out[m * P : (m + 1) * P, :], in_=res[:])
+
+        for h in range(2):
+            nc.vector.tensor_copy(windows[0][:].indirect(offsets[:, 8 * h : 8 * h + 8]), gv[:, 0, h * P : (h + 1) * P])
+        scatter(1)
+        y0 = fade_turned(0)
+        add_and_store(0, turn_back(y0, 0, (6, 7)))
+        scatter(2)
+        add_and_store(1, turn_back(y0, 1, (0, 1)))
+        scatter(3)
+        y1 = fade_turned(1)
+        add_and_store(2, turn_back(y1, 2, (2, 3)))
+        add_and_store(3, turn_back(y1, 3, (6, 7)))

@@ -54,7 +54,7 @@ def tile_attend_bmixednorm_v_kernel(tc, query, keys_words, keys_scales, share, q
         fade_rows = sb.tile([P, P], F32, name="fade_rows")
         nc.vector.memset(fade_rows[:], 0.0)
         nc.sync.dma_start(out=fade_rows[0 : T // P, :], in_=fade.rearrange("o (b t) -> (o b) t", t=P))
-        g_raw = sb.tile([P, PACK, E], F32, name="g_raw")
+        g_raw = sb.tile([P, PACK, E], F32, name="g_raw", tag="g_raw_then_fade")
         nc.sync.dma_start(out=g_raw[:], in_=grows.rearrange("(p r) e -> p r e", r=PACK))
         old_rows = old.rearrange("(m p) t -> p m t", p=P)
         old_sb = []
@@ -66,9 +66,9 @@ def tile_attend_bmixednorm_v_kernel(tc, query, keys_words, keys_scales, share, q
         ident = sb.tile([P, P], F32, name="ident")
         make_identity(nc, ident[:])
         windows = []
-        for m in range(2):
+        for m in range(3):
             w = sb.tile([P, T], F32, name="window%d" % m)
-            nc.vector.memset(w[:], 0.0)
+            (nc.vector if m < 2 else nc.gpsimd).memset(w[:], 0.0)
             windows.append(w)
 
         kg_bytes = sb.tile([P, I], U8, name="kg_bytes", align_bytes=64)
@@ -131,8 +131,6 @@ def tile_attend_bmixednorm_v_kernel(tc, query, keys_words, keys_scales, share, q
             )
 
         g_bf = sb.tile([P, E, PACK], BF16, name="g_bf", tag="neg_max_then_g_bf", align_bytes=64)
-        g_words = sb.tile([P, E], U32, name="g_words", align_bytes=64)
-        g_bytes = sb.tile([P, E], U8, name="g_bytes", align_bytes=64)
         for m in range(E // P):
             cols = slice(m * P, (m + 1) * P)
             nc.scalar.copy(
@@ -143,20 +141,23 @@ def tile_attend_bmixednorm_v_kernel(tc, query, keys_words, keys_scales, share, q
         w_words = sb.tile([P, I], U32, name="w_words", align_bytes=64)
         w_bytes = sb.tile([P, I], U8, name="w_bytes", align_bytes=64)
         gv = sb.tile([P, E // P, I], F32, name="gv")
+        g_bytes = sb.tile([P, E], U8, name="g_bytes", align_bytes=64)
+
+        def quantize_grows(words, first, count):
+            nc.vector.quantize_mx(
+                out=words.bitcast(FP8X4),
+                scales=g_bytes[:, first : first + count],
+                in_=g_bf[:, first : first + count, :].rearrange("p e r -> p (e r)"),
+            )
+
+        g_first = sb.tile([P, P], U32, name="g_first", align_bytes=64)
+        quantize_grows(g_first[:], 0, P)
         for h in range(2):
             gs = slice(h * (G // 2), (h + 1) * (G // 2))
             slots = slice(h * P, (h + 1) * P)
-            v = sb.tile([P, G // 2, PACK], F32, name="v%d" % h, tag="stage%d" % h, align_bytes=64)
-            w_bf = sb.tile([P, P, PACK], BF16, name="w_bf%d" % h, tag="stage%d" % (h + 1), align_bytes=64)
+            v = sb.tile([P, G // 2, PACK], F32, name="v%d" % h)
+            w_bf = sb.tile([P, P, PACK], BF16, name="w_bf%d" % h, tag="w_bf%d" % h, align_bytes=64)
             nc.vector.reciprocal(v[:].rearrange("p g r -> p r g"), den[:, :, gs])
-            if h == 0:
-                for m in range(E // P):
-                    cols = slice(m * P, (m + 1) * P)
-                    nc.vector.quantize_mx(
-                        out=g_words[:, cols].bitcast(FP8X4),
-                        scales=g_bytes[:, cols],
-                        in_=g_bf[:, cols, :].rearrange("p e r -> p (e r)"),
-                    )
             nc.vector.tensor_tensor(
                 w_bf[:].rearrange("p (g j) r -> p g j r", j=GROUP),
                 p_sb[:, :, slots].rearrange("p r (g j) -> p g j r", j=GROUP),
@@ -168,21 +169,36 @@ def tile_attend_bmixednorm_v_kernel(tc, query, keys_words, keys_scales, share, q
                 scales=w_bytes[:, slots],
                 in_=w_bf[:].rearrange("p i r -> p (i r)"),
             )
-            first = bank(2 * h, "gv_first%d" % h)
-            others = bank(2 * h + 1, "gv_others%d" % h)
-            for m in range(E // P):
-                cols = slice(m * P, (m + 1) * P)
-                nc.tensor.matmul_mx(
-                    out=first[:, 0:P] if m == 0 else others[:, (m - 1) * P : m * P],
-                    lhsT=g_words[:, cols].bitcast(FP8X4),
-                    lhsT_scale=g_bytes[:, cols],
-                    rhs=w_words[:, slots].bitcast(FP8X4),
-                    rhs_scale=w_bytes[:, slots],
-                    start=True,
-                    stop=True,
-                )
+            first = bank(2 + h, "gv_first%d" % h)
+            nc.tensor.matmul_mx(
+                out=first[:, 0:P],
+                lhsT=g_first[:].bitcast(FP8X4),
+                lhsT_scale=g_bytes[:, 0:P],
+                rhs=w_words[:, slots].bitcast(FP8X4),
+                rhs_scale=w_bytes[:, slots],
+                start=True,
+                stop=True,
+            )
             nc.scalar.copy(out=gv[:, 0, slots], in_=first[:, 0:P])
-            nc.scalar.copy(out=gv[:, 1:, slots], in_=others[:, 0 : 3 * P].rearrange("p (m i) -> p m i", i=P))
+        g_rest = sb.tile([P, E - P], U32, name="g_rest", tag="w_bf0", align_bytes=64)
+        quantize_grows(g_rest[:, 0:P], P, P)
+        quantize_grows(g_rest[:, P : 3 * P], 2 * P, 2 * P)
+        for m in range(1, E // P):
+            if m != 3:
+                others = bank(3 + m, "gv_others%d" % m)
+            at = slice(I, 2 * I) if m == 3 else slice(0, I)
+            nc.tensor.matmul_mx(
+                out=others[:, at],
+                lhsT=g_rest[:, (m - 1) * P : m * P].bitcast(FP8X4),
+                lhsT_scale=g_bytes[:, m * P : (m + 1) * P],
+                rhs=w_words[:].bitcast(FP8X4),
+                rhs_scale=w_bytes[:],
+                start=True,
+                stop=True,
+            )
+            if m == 1:
+                nc.scalar.copy(out=gv[:, 1, :], in_=others[:, 0:I])
+        nc.scalar.copy(out=gv[:, 2:4, :], in_=others[:].rearrange("p (m i) -> p m i", i=I))
 
         fade_ps = bank(6, "fade_ps")
         nc.tensor.transpose(fade_ps[:, 0:P], fade_rows[:], ident[:])
@@ -192,7 +208,7 @@ def tile_attend_bmixednorm_v_kernel(tc, query, keys_words, keys_scales, share, q
         def fade_turned(pair):
             y = sb.tile([P, T // P, 2 * P], F32, name="faded_t%d" % pair)
             for b2 in range(T // P // 2):
-                turned = bank(4 + b2 % 2, "turned%d_%d" % (pair, b2))
+                turned = bank(6 + b2 % 2, "turned%d_%d" % (pair, b2))
                 for k in range(2):
                     b = 2 * b2 + k
                     for m in range(2):
@@ -216,26 +232,46 @@ def tile_attend_bmixednorm_v_kernel(tc, query, keys_words, keys_scales, share, q
             return backs
 
         def scatter(m):
-            nc.vector.tensor_copy(windows[m % 2][:].indirect(offsets[:]), gv[:, m, :])
+            nc.vector.tensor_copy(windows[min(m, 2)][:].indirect(offsets[:]), gv[:, m, :])
 
         def add_and_store(m, backs):
             res = sb.tile([P, T], F32, name="res%d" % m)
             for h in range(2):
                 cols = slice(h * BANK, (h + 1) * BANK)
-                nc.vector.tensor_tensor(res[:, cols], backs[h][:], windows[m % 2][:, cols], ALU.add)
+                nc.vector.tensor_tensor(res[:, cols], backs[h][:], windows[min(m, 2)][:, cols], ALU.add)
                 if m == E // P - 1:
                     nc.sync.dma_start(out=out[m * P : (m + 1) * P, cols], in_=res[:, cols])
             if m < E // P - 1:
                 nc.sync.dma_start(out=out[m * P : (m + 1) * P, :], in_=res[:])
 
+        fade_all = sb.tile([P, T], F32, name="fade_all", tag="g_raw_then_fade")
+        for h in range(2):
+            spread = bank(h, "spread%d" % h)
+            for k in range(4):
+                b = 4 * h + k
+                nc.tensor.transpose(spread[:, k * P : (k + 1) * P], fade_cols[:, b : b + 1].to_broadcast([P, P]), ident[:])
+            nc.scalar.copy(out=fade_all[:, h * BANK : (h + 1) * BANK], in_=spread[:])
+
         for h in range(2):
             nc.vector.tensor_copy(windows[0][:].indirect(offsets[:, 8 * h : 8 * h + 8]), gv[:, 0, h * P : (h + 1) * P])
         scatter(1)
-        y0 = fade_turned(0)
-        add_and_store(0, turn_back(y0, 0, (6, 7)))
         scatter(2)
-        add_and_store(1, turn_back(y0, 1, (0, 1)))
-        scatter(3)
         y1 = fade_turned(1)
-        add_and_store(2, turn_back(y1, 2, (2, 3)))
-        add_and_store(3, turn_back(y1, 3, (6, 7)))
+        late = []
+        for m in range(2):
+            faded = sb.tile([P, T], F32, name="faded%d" % m, tag="w_bf1", align_bytes=64)
+            nc.gpsimd.tensor_tensor(faded[:], old_sb[0][:, m, :], fade_all[:], ALU.mult)
+            res = sb.tile([P, T], F32, name="res%d" % m)
+            if m == 0:
+                nc.gpsimd.tensor_tensor(res[:], faded[:], windows[m][:], ALU.add)
+                nc.sync.dma_start(out=out[m * P : (m + 1) * P, :], in_=res[:])
+            else:
+                for h in range(2):
+                    cols = slice(h * BANK, (h + 1) * BANK)
+                    nc.gpsimd.tensor_tensor(res[:, cols], faded[:, cols], windows[m][:, cols], ALU.add)
+                    late.append((out[m * P : (m + 1) * P, cols], res[:, cols]))
+        add_and_store(2, turn_back(y1, 2, (0, 1)))
+        scatter(3)
+        add_and_store(3, turn_back(y1, 3, (2, 3)))
+        for dst, src in late:
+            nc.scalar.dma_start(out=dst, in_=src)

@@ -36,6 +36,8 @@ def tile_attend_bmixednorm_v_kernel(tc, query, keys_words, keys_scales, share, q
         key_bytes = sb.tile([P, T], U8, name="key_bytes", align_bytes=64)
         nc.gpsimd.memset(key_bytes[:].bitcast(I32), 0)
         nc.sync.dma_start(offsets[:], offs)
+        fade_runs = sb.tile([P, T // P], F32, name="fade_runs", tag="fade_runs_then_q_bytes", align_bytes=64)
+        nc.sync.dma_start(out=fade_runs[:], in_=fade.rearrange("o (p j) -> (o p) j", p=P))
         query_rows = query.rearrange("(p j) q -> p j q", j=PACK)
         q_raw = [sb.tile([P, PACK, Q // 2], F32, name="q_raw%d" % h) for h in range(2)]
         nc.sync.dma_start(out=q_raw[0][:], in_=query_rows[:, :, 0 : Q // 2])
@@ -51,25 +53,32 @@ def tile_attend_bmixednorm_v_kernel(tc, query, keys_words, keys_scales, share, q
         nc.sync.dma_start(out=share_sb[:], in_=share.rearrange("(p r) o -> p (r o)", r=PACK))
         qs_sb = sb.tile([P, PACK], F32, name="qs_sb")
         nc.sync.dma_start(out=qs_sb[:], in_=qs.rearrange("(p r) o -> p (r o)", r=PACK))
-        fade_rows = sb.tile([P, P], F32, name="fade_rows")
-        nc.vector.memset(fade_rows[:], 0.0)
-        nc.sync.dma_start(out=fade_rows[0 : T // P, :], in_=fade.rearrange("o (b t) -> (o b) t", t=P))
-        g_raw = sb.tile([P, PACK, E], F32, name="g_raw", tag="g_raw_then_fade")
+        g_raw = sb.tile([P, PACK, E], F32, name="g_raw", tag="g_raw_then_faded_t")
         nc.sync.dma_start(out=g_raw[:], in_=grows.rearrange("(p r) e -> p r e", r=PACK))
         old_rows = old.rearrange("(m p) t -> p m t", p=P)
-        old_sb = []
+        old_sb = [sb.tile([P, 2, T], F32, name="old%d" % h) for h in range(2)]
         for h in range(2):
-            t = sb.tile([P, 2, T], F32, name="old%d" % h)
-            nc.sync.dma_start(out=t[:], in_=old_rows[:, 2 * h : 2 * h + 2, :])
-            old_sb.append(t)
+            nc.sync.dma_start(out=old_sb[h][:], in_=old_rows[:, 2 * h : 2 * h + 2, :])
 
         ident = sb.tile([P, P], F32, name="ident")
         make_identity(nc, ident[:])
         windows = []
         for m in range(3):
             w = sb.tile([P, T], F32, name="window%d" % m)
-            (nc.vector if m < 2 else nc.gpsimd).memset(w[:], 0.0)
+            (nc.vector if m == 0 else nc.gpsimd).memset(w[:], 0.0)
             windows.append(w)
+
+        fade_all = sb.tile([P, T], F32, name="fade_all")
+        for h in range(2):
+            spread = bank(h, "spread%d" % h)
+            for k in range(4):
+                j = 4 * h + k
+                nc.tensor.transpose(spread[:, k * P : (k + 1) * P], fade_runs[:, j : j + 1].to_broadcast([P, P]), ident[:])
+            nc.scalar.activation(
+                fade_all[:].rearrange("p (n j) -> p n j", j=T // P)[:, :, 4 * h : 4 * h + 4],
+                spread[:].rearrange("p (k n) -> p n k", n=P),
+                ACT.Copy,
+            )
 
         kg_bytes = sb.tile([P, I], U8, name="kg_bytes", align_bytes=64)
         nc.vector.tensor_copy(kg_bytes[:], key_bytes[:].indirect(offsets[:]))
@@ -81,10 +90,10 @@ def tile_attend_bmixednorm_v_kernel(tc, query, keys_words, keys_scales, share, q
                 in_=q_raw[h][:].rearrange("p j (s r) -> p s j r", r=PACK),
             )
         q_words = sb.tile([P, Q], U32, name="q_words", align_bytes=64)
-        q_bytes = sb.tile([P, Q], U8, name="q_bytes", align_bytes=64)
-        neg_max = sb.tile([P, PACK], F32, name="neg_max", tag="neg_max_then_g_bf", align_bytes=64)
+        q_bytes = sb.tile([P, Q], U8, name="q_bytes", tag="fade_runs_then_q_bytes", align_bytes=64)
+        neg_max = sb.tile([P, PACK], F32, name="neg_max")
         p_sb = sb.tile([P, PACK, I], F32, name="p_sb")
-        z = sb.tile([P, PACK], F32, name="z")
+        z_mix = sb.tile([P, PACK], F32, name="z_mix")
         nc.vector.quantize_mx(
             out=q_words[:].bitcast(FP8X4), scales=q_bytes[:], in_=q_bf[:].rearrange("p r s j -> p (r s j)")
         )
@@ -116,27 +125,34 @@ def tile_attend_bmixednorm_v_kernel(tc, query, keys_words, keys_scales, share, q
 
         for r in range(PACK):
             nc.vector.tensor_reduce(neg_max[:, r : r + 1], scores[r][:, 0:I], AX.X, ALU.max, negate=True)
-            nc.scalar.activation(
-                p_sb[:, r, :], scores[r][:, 0:I], ACT.Exp, bias=neg_max[:, r : r + 1], accum_out=z[:, r : r + 1]
-            )
-        s = sb.tile([P, PACK, G], F32, name="s")
+            nc.scalar.activation(p_sb[:, r, :], scores[r][:, 0:I], ACT.Exp, bias=neg_max[:, r : r + 1])
+        s = sb.tile([P, PACK, G], F32, name="s", tag="s_then_g_bf0", align_bytes=64)
+        den = sb.tile([P, PACK, G], F32, name="den")
+        v = sb.tile([P, G, PACK], F32, name="v")
         for r in range(PACK):
             nc.vector.tensor_reduce(s[:, r, :], p_sb[:, r, :].rearrange("p (g j) -> p g j", j=GROUP), AX.X, ALU.add)
-        z_mix = sb.tile([P, PACK], F32, name="z_mix")
-        nc.vector.tensor_tensor(z_mix[:], z[:], row_mix[:], ALU.mult)
-        den = sb.tile([P, PACK, G], F32, name="den")
-        for r in range(PACK):
-            nc.vector.tensor_scalar(
-                den[:, r, :], s[:, r, :], group_mix[:, r : r + 1], z_mix[:, r : r + 1], ALU.mult, ALU.add
+            nc.scalar.activation(
+                den[:, r, :], s[:, r, :], ACT.Copy, scale=row_mix[:, r : r + 1], accum_out=z_mix[:, r : r + 1]
             )
+            nc.scalar.activation(
+                den[:, r, :], s[:, r, :], ACT.Identity, bias=z_mix[:, r : r + 1], scale=group_mix[:, r : r + 1]
+            )
+        for r in range(PACK):
+            nc.vector.reciprocal(v[:, :, r], den[:, r, :])
 
-        g_bf = sb.tile([P, E, PACK], BF16, name="g_bf", tag="neg_max_then_g_bf", align_bytes=64)
-        for m in range(E // P):
+        g_bf = [
+            sb.tile([P, E // 2, PACK], BF16, name="g_bf0", tag="s_then_g_bf0", align_bytes=64),
+            sb.tile([P, E // 2, PACK], BF16, name="g_bf1", tag="g_bf1_then_faded", align_bytes=64),
+        ]
+        for m in range(2):
             cols = slice(m * P, (m + 1) * P)
             nc.scalar.copy(
-                out=g_bf[:, cols, :].rearrange("p (c i) r -> p c r i", i=4),
+                out=g_bf[0][:, cols, :].rearrange("p (c i) r -> p c r i", i=4),
                 in_=g_raw[:, :, cols].rearrange("p r (c i) -> p c r i", i=4),
             )
+        nc.gpsimd.tensor_scalar(
+            g_bf[1][:], g_raw[:, :, E // 2 : E].rearrange("p r e -> p e r"), 1.0, 0.0, ALU.mult, ALU.add
+        )
 
         w_words = sb.tile([P, I], U32, name="w_words", align_bytes=64)
         w_bytes = sb.tile([P, I], U8, name="w_bytes", align_bytes=64)
@@ -147,7 +163,7 @@ def tile_attend_bmixednorm_v_kernel(tc, query, keys_words, keys_scales, share, q
             nc.vector.quantize_mx(
                 out=words.bitcast(FP8X4),
                 scales=g_bytes[:, first : first + count],
-                in_=g_bf[:, first : first + count, :].rearrange("p e r -> p (e r)"),
+                in_=g_bf[first // (E // 2)][:, first % (E // 2) : first % (E // 2) + count, :].rearrange("p e r -> p (e r)"),
             )
 
         g_first = sb.tile([P, P], U32, name="g_first", align_bytes=64)
@@ -155,15 +171,15 @@ def tile_attend_bmixednorm_v_kernel(tc, query, keys_words, keys_scales, share, q
         for h in range(2):
             gs = slice(h * (G // 2), (h + 1) * (G // 2))
             slots = slice(h * P, (h + 1) * P)
-            v = sb.tile([P, G // 2, PACK], F32, name="v%d" % h)
             w_bf = sb.tile([P, P, PACK], BF16, name="w_bf%d" % h, tag="w_bf%d" % h, align_bytes=64)
-            nc.vector.reciprocal(v[:].rearrange("p g r -> p r g"), den[:, :, gs])
-            nc.vector.tensor_tensor(
-                w_bf[:].rearrange("p (g j) r -> p g j r", j=GROUP),
-                p_sb[:, :, slots].rearrange("p r (g j) -> p g j r", j=GROUP),
-                v[:].unsqueeze(2).to_broadcast([P, G // 2, GROUP, PACK]),
-                ALU.mult,
-            )
+            for k in range(2):
+                run = slice(4 * k, 4 * k + 4)
+                nc.vector.tensor_tensor(
+                    w_bf[:].rearrange("p (g j) r -> p g r j", j=GROUP)[:, :, :, run],
+                    p_sb[:, :, slots].rearrange("p r (g j) -> p g r j", j=GROUP)[:, :, :, run],
+                    v[:, gs, :].unsqueeze(3).to_broadcast([P, G // 2, PACK, 4]),
+                    ALU.mult,
+                )
             nc.vector.quantize_mx(
                 out=w_words[:, slots].bitcast(FP8X4),
                 scales=w_bytes[:, slots],
@@ -180,7 +196,7 @@ def tile_attend_bmixednorm_v_kernel(tc, query, keys_words, keys_scales, share, q
                 stop=True,
             )
             nc.scalar.copy(out=gv[:, 0, slots], in_=first[:, 0:P])
-        g_rest = sb.tile([P, E - P], U32, name="g_rest", tag="w_bf0", align_bytes=64)
+        g_rest = sb.tile([P, E - P], U32, name="g_rest", tag="w_bf1", align_bytes=64)
         quantize_grows(g_rest[:, 0:P], P, P)
         quantize_grows(g_rest[:, P : 3 * P], 2 * P, 2 * P)
         for m in range(1, E // P):
@@ -200,15 +216,18 @@ def tile_attend_bmixednorm_v_kernel(tc, query, keys_words, keys_scales, share, q
                 nc.scalar.copy(out=gv[:, 1, :], in_=others[:, 0:I])
         nc.scalar.copy(out=gv[:, 2:4, :], in_=others[:].rearrange("p (m i) -> p m i", i=I))
 
-        fade_ps = bank(6, "fade_ps")
-        nc.tensor.transpose(fade_ps[:, 0:P], fade_rows[:], ident[:])
         fade_cols = sb.tile([P, T // P], F32, name="fade_cols")
-        nc.vector.tensor_copy(fade_cols[:], fade_ps[:, 0 : T // P])
+        for h in range(2):
+            turned_fade = bank(6 + h, "turned_fade%d" % h)
+            for k in range(4):
+                b = 4 * h + k
+                nc.tensor.transpose(turned_fade[:, k * P : (k + 1) * P], fade_all[:, b * P : (b + 1) * P], ident[:])
+            nc.scalar.activation(fade_cols[:, 4 * h : 4 * h + 4], turned_fade[:, 0:BANK:P], ACT.Copy)
 
         def fade_turned(pair):
-            y = sb.tile([P, T // P, 2 * P], F32, name="faded_t%d" % pair)
+            y = sb.tile([P, T // P, 2 * P], F32, name="faded_t%d" % pair, tag="g_raw_then_faded_t")
             for b2 in range(T // P // 2):
-                turned = bank(6 + b2 % 2, "turned%d_%d" % (pair, b2))
+                turned = bank((6, 7, 2, 3)[b2], "turned%d_%d" % (pair, b2))
                 for k in range(2):
                     b = 2 * b2 + k
                     for m in range(2):
@@ -236,21 +255,16 @@ def tile_attend_bmixednorm_v_kernel(tc, query, keys_words, keys_scales, share, q
 
         def add_and_store(m, backs):
             res = sb.tile([P, T], F32, name="res%d" % m)
-            for h in range(2):
-                cols = slice(h * BANK, (h + 1) * BANK)
-                nc.vector.tensor_tensor(res[:, cols], backs[h][:], windows[min(m, 2)][:, cols], ALU.add)
+            pieces = (0, 512, 768, 1024) if m == E // P - 1 else (0, 512, 1024)
+            for lo, hi in zip(pieces, pieces[1:]):
+                cols = slice(lo, hi)
+                nc.vector.tensor_tensor(
+                    res[:, cols], backs[lo // BANK][:, lo % BANK : lo % BANK + hi - lo], windows[min(m, 2)][:, cols], ALU.add
+                )
                 if m == E // P - 1:
                     nc.sync.dma_start(out=out[m * P : (m + 1) * P, cols], in_=res[:, cols])
             if m < E // P - 1:
                 nc.sync.dma_start(out=out[m * P : (m + 1) * P, :], in_=res[:])
-
-        fade_all = sb.tile([P, T], F32, name="fade_all", tag="g_raw_then_fade")
-        for h in range(2):
-            spread = bank(h, "spread%d" % h)
-            for k in range(4):
-                b = 4 * h + k
-                nc.tensor.transpose(spread[:, k * P : (k + 1) * P], fade_cols[:, b : b + 1].to_broadcast([P, P]), ident[:])
-            nc.scalar.copy(out=fade_all[:, h * BANK : (h + 1) * BANK], in_=spread[:])
 
         for h in range(2):
             nc.vector.tensor_copy(windows[0][:].indirect(offsets[:, 8 * h : 8 * h + 8]), gv[:, 0, h * P : (h + 1) * P])
@@ -259,7 +273,7 @@ def tile_attend_bmixednorm_v_kernel(tc, query, keys_words, keys_scales, share, q
         y1 = fade_turned(1)
         late = []
         for m in range(2):
-            faded = sb.tile([P, T], F32, name="faded%d" % m, tag="w_bf1", align_bytes=64)
+            faded = sb.tile([P, T], F32, name="faded%d" % m, tag="g_bf1_then_faded", align_bytes=64)
             nc.gpsimd.tensor_tensor(faded[:], old_sb[0][:, m, :], fade_all[:], ALU.mult)
             res = sb.tile([P, T], F32, name="res%d" % m)
             if m == 0:
@@ -270,8 +284,8 @@ def tile_attend_bmixednorm_v_kernel(tc, query, keys_words, keys_scales, share, q
                     cols = slice(h * BANK, (h + 1) * BANK)
                     nc.gpsimd.tensor_tensor(res[:, cols], faded[:, cols], windows[m][:, cols], ALU.add)
                     late.append((out[m * P : (m + 1) * P, cols], res[:, cols]))
-        add_and_store(2, turn_back(y1, 2, (0, 1)))
+        add_and_store(2, turn_back(y1, 2, (6, 7)))
         scatter(3)
-        add_and_store(3, turn_back(y1, 3, (2, 3)))
+        add_and_store(3, turn_back(y1, 3, (0, 1)))
         for dst, src in late:
             nc.scalar.dma_start(out=dst, in_=src)

@@ -53,12 +53,12 @@ def tile_attend_bmixednorm_v_kernel(tc, query, keys_words, keys_scales, share, q
         nc.sync.dma_start(out=share_sb[:], in_=share.rearrange("(p r) o -> p (r o)", r=PACK))
         qs_sb = sb.tile([P, PACK], F32, name="qs_sb")
         nc.sync.dma_start(out=qs_sb[:], in_=qs.rearrange("(p r) o -> p (r o)", r=PACK))
-        g_raw = sb.tile([P, PACK, E], F32, name="g_raw", tag="g_raw_then_faded_t")
+        old_sb = [sb.tile([P, T], F32, name="old%d" % m) for m in range(E // P)]
+        nc.sync.dma_start(out=old_sb[0][:], in_=old[0:P, :])
+        g_raw = sb.tile([P, PACK, E], F32, name="g_raw")
         nc.sync.dma_start(out=g_raw[:], in_=grows.rearrange("(p r) e -> p r e", r=PACK))
-        old_rows = old.rearrange("(m p) t -> p m t", p=P)
-        old_sb = [sb.tile([P, 2, T], F32, name="old%d" % h) for h in range(2)]
-        for h in range(2):
-            nc.sync.dma_start(out=old_sb[h][:], in_=old_rows[:, 2 * h : 2 * h + 2, :])
+        for m in range(1, E // P):
+            nc.sync.dma_start(out=old_sb[m][:], in_=old[m * P : (m + 1) * P, :])
 
         ident = sb.tile([P, P], F32, name="ident")
         make_identity(nc, ident[:])
@@ -126,7 +126,7 @@ def tile_attend_bmixednorm_v_kernel(tc, query, keys_words, keys_scales, share, q
         for r in range(PACK):
             nc.vector.tensor_reduce(neg_max[:, r : r + 1], scores[r][:, 0:I], AX.X, ALU.max, negate=True)
             nc.scalar.activation(p_sb[:, r, :], scores[r][:, 0:I], ACT.Exp, bias=neg_max[:, r : r + 1])
-        s = sb.tile([P, PACK, G], F32, name="s", tag="s_then_g_bf0", align_bytes=64)
+        s = sb.tile([P, PACK, G], F32, name="s", tag="s_then_g_bf_then_faded", align_bytes=64)
         den = sb.tile([P, PACK, G], F32, name="den")
         v = sb.tile([P, G, PACK], F32, name="v")
         for r in range(PACK):
@@ -140,19 +140,13 @@ def tile_attend_bmixednorm_v_kernel(tc, query, keys_words, keys_scales, share, q
         for r in range(PACK):
             nc.vector.reciprocal(v[:, :, r], den[:, r, :])
 
-        g_bf = [
-            sb.tile([P, E // 2, PACK], BF16, name="g_bf0", tag="s_then_g_bf0", align_bytes=64),
-            sb.tile([P, E // 2, PACK], BF16, name="g_bf1", tag="g_bf1_then_faded", align_bytes=64),
-        ]
-        for m in range(2):
+        g_bf = sb.tile([P, E, PACK], BF16, name="g_bf", tag="s_then_g_bf_then_faded", align_bytes=64)
+        for m in range(E // P):
             cols = slice(m * P, (m + 1) * P)
             nc.scalar.copy(
-                out=g_bf[0][:, cols, :].rearrange("p (c i) r -> p c r i", i=4),
+                out=g_bf[:, cols, :].rearrange("p (c i) r -> p c r i", i=4),
                 in_=g_raw[:, :, cols].rearrange("p r (c i) -> p c r i", i=4),
             )
-        nc.gpsimd.tensor_scalar(
-            g_bf[1][:], g_raw[:, :, E // 2 : E].rearrange("p r e -> p e r"), 1.0, 0.0, ALU.mult, ALU.add
-        )
 
         w_words = sb.tile([P, I], U32, name="w_words", align_bytes=64)
         w_bytes = sb.tile([P, I], U8, name="w_bytes", align_bytes=64)
@@ -163,7 +157,7 @@ def tile_attend_bmixednorm_v_kernel(tc, query, keys_words, keys_scales, share, q
             nc.vector.quantize_mx(
                 out=words.bitcast(FP8X4),
                 scales=g_bytes[:, first : first + count],
-                in_=g_bf[first // (E // 2)][:, first % (E // 2) : first % (E // 2) + count, :].rearrange("p e r -> p (e r)"),
+                in_=g_bf[:, first : first + count, :].rearrange("p e r -> p (e r)"),
             )
 
         g_first = sb.tile([P, P], U32, name="g_first", align_bytes=64)
@@ -224,29 +218,21 @@ def tile_attend_bmixednorm_v_kernel(tc, query, keys_words, keys_scales, share, q
                 nc.tensor.transpose(turned_fade[:, k * P : (k + 1) * P], fade_all[:, b * P : (b + 1) * P], ident[:])
             nc.scalar.activation(fade_cols[:, 4 * h : 4 * h + 4], turned_fade[:, 0:BANK:P], ACT.Copy)
 
-        def fade_turned(pair):
-            y = sb.tile([P, T // P, 2 * P], F32, name="faded_t%d" % pair, tag="g_raw_then_faded_t")
-            for b2 in range(T // P // 2):
-                turned = bank((6, 7, 2, 3)[b2], "turned%d_%d" % (pair, b2))
-                for k in range(2):
-                    b = 2 * b2 + k
-                    for m in range(2):
-                        nc.tensor.transpose(
-                            turned[:, (2 * k + m) * P : (2 * k + m + 1) * P], old_sb[pair][:, m, b * P : (b + 1) * P], ident[:]
-                        )
-                for k in range(2):
-                    b = 2 * b2 + k
-                    nc.scalar.activation(
-                        y[:, b, :], turned[:, 2 * k * P : (2 * k + 2) * P], ACT.Copy, scale=fade_cols[:, b : b + 1]
-                    )
-            return y
-
-        def turn_back(y, m, banks):
+        def faded_old_in_psum(m, turn_banks, back_banks):
+            y = sb.tile([P, T // P, P], F32, name="faded_t%d" % m)
             backs = []
             for h in range(2):
-                back = bank(banks[h], "back%d_%d" % (m, h))
+                turned = bank(turn_banks[h], "turned%d_%d" % (m, h))
                 for k in range(4):
-                    nc.tensor.transpose(back[:, k * P : (k + 1) * P], y[:, 4 * h + k, (m % 2) * P : (m % 2 + 1) * P], ident[:])
+                    b = 4 * h + k
+                    nc.tensor.transpose(turned[:, k * P : (k + 1) * P], old_sb[m][:, b * P : (b + 1) * P], ident[:])
+                for k in range(4):
+                    b = 4 * h + k
+                    nc.scalar.activation(y[:, b, :], turned[:, k * P : (k + 1) * P], ACT.Copy, scale=fade_cols[:, b : b + 1])
+            for h in range(2):
+                back = bank(back_banks[h], "back%d_%d" % (m, h))
+                for k in range(4):
+                    nc.tensor.transpose(back[:, k * P : (k + 1) * P], y[:, 4 * h + k, :], ident[:])
                 backs.append(back)
             return backs
 
@@ -270,11 +256,10 @@ def tile_attend_bmixednorm_v_kernel(tc, query, keys_words, keys_scales, share, q
             nc.vector.tensor_copy(windows[0][:].indirect(offsets[:, 8 * h : 8 * h + 8]), gv[:, 0, h * P : (h + 1) * P])
         scatter(1)
         scatter(2)
-        y1 = fade_turned(1)
         late = []
         for m in range(2):
-            faded = sb.tile([P, T], F32, name="faded%d" % m, tag="g_bf1_then_faded", align_bytes=64)
-            nc.gpsimd.tensor_tensor(faded[:], old_sb[0][:, m, :], fade_all[:], ALU.mult)
+            faded = sb.tile([P, T], F32, name="faded%d" % m, tag=("faded0", "s_then_g_bf_then_faded")[m], align_bytes=64)
+            nc.gpsimd.tensor_tensor(faded[:], old_sb[m][:], fade_all[:], ALU.mult)
             res = sb.tile([P, T], F32, name="res%d" % m)
             if m == 0:
                 nc.gpsimd.tensor_tensor(res[:], faded[:], windows[m][:], ALU.add)
@@ -284,8 +269,8 @@ def tile_attend_bmixednorm_v_kernel(tc, query, keys_words, keys_scales, share, q
                     cols = slice(h * BANK, (h + 1) * BANK)
                     nc.gpsimd.tensor_tensor(res[:, cols], faded[:, cols], windows[m][:, cols], ALU.add)
                     late.append((out[m * P : (m + 1) * P, cols], res[:, cols]))
-        add_and_store(2, turn_back(y1, 2, (6, 7)))
+        add_and_store(2, faded_old_in_psum(2, (2, 3), (6, 7)))
         scatter(3)
-        add_and_store(3, turn_back(y1, 3, (0, 1)))
+        add_and_store(3, faded_old_in_psum(3, (4, 5), (0, 1)))
         for dst, src in late:
             nc.scalar.dma_start(out=dst, in_=src)

@@ -63,9 +63,9 @@ def tile_attend_bmixednorm_v_kernel(tc, query, keys_words, keys_scales, share, q
         ident = sb.tile([P, P], F32, name="ident")
         make_identity(nc, ident[:])
         windows = []
-        for m in range(3):
+        for m in range(E // P):
             w = sb.tile([P, T], F32, name="window%d" % m)
-            (nc.vector if m == 0 else nc.gpsimd).memset(w[:], 0.0)
+            (nc.vector if m < 3 else nc.gpsimd).memset(w[:], 0.0)
             windows.append(w)
 
         fade_all = sb.tile([P, T], F32, name="fade_all")
@@ -218,59 +218,42 @@ def tile_attend_bmixednorm_v_kernel(tc, query, keys_words, keys_scales, share, q
                 nc.tensor.transpose(turned_fade[:, k * P : (k + 1) * P], fade_all[:, b * P : (b + 1) * P], ident[:])
             nc.scalar.activation(fade_cols[:, 4 * h : 4 * h + 4], turned_fade[:, 0:BANK:P], ACT.Copy)
 
-        def faded_old_in_psum(m, turn_banks, back_banks):
-            y = sb.tile([P, T // P, P], F32, name="faded_t%d" % m)
-            backs = []
+        for h in range(2):
+            nc.vector.tensor_copy(windows[0][:].indirect(offsets[:, 8 * h : 8 * h + 8]), gv[:, 0, h * P : (h + 1) * P])
+        for m in range(1, E // P):
+            nc.vector.tensor_copy(windows[m][:].indirect(offsets[:]), gv[:, m, :])
+
+        faded_t = {}
+        for m, banks in ((2, (2, 3)), (3, (4, 5))):
+            faded_t[m] = sb.tile([P, T // P, P], F32, name="faded_t%d" % m)
             for h in range(2):
-                turned = bank(turn_banks[h], "turned%d_%d" % (m, h))
+                turned = bank(banks[h], "turned%d_%d" % (m, h))
                 for k in range(4):
                     b = 4 * h + k
                     nc.tensor.transpose(turned[:, k * P : (k + 1) * P], old_sb[m][:, b * P : (b + 1) * P], ident[:])
                 for k in range(4):
                     b = 4 * h + k
-                    nc.scalar.activation(y[:, b, :], turned[:, k * P : (k + 1) * P], ACT.Copy, scale=fade_cols[:, b : b + 1])
+                    nc.scalar.activation(
+                        faded_t[m][:, b, :], turned[:, k * P : (k + 1) * P], ACT.Copy, scale=fade_cols[:, b : b + 1]
+                    )
+        for m, banks, pieces in ((2, (6, 7), (0, 512, 1024)), (3, (0, 1), (0, 512, 768, 1024))):
+            backs = []
             for h in range(2):
-                back = bank(back_banks[h], "back%d_%d" % (m, h))
+                back = bank(banks[h], "back%d_%d" % (m, h))
                 for k in range(4):
-                    nc.tensor.transpose(back[:, k * P : (k + 1) * P], y[:, 4 * h + k, :], ident[:])
+                    nc.tensor.transpose(back[:, k * P : (k + 1) * P], faded_t[m][:, 4 * h + k, :], ident[:])
                 backs.append(back)
-            return backs
-
-        def scatter(m):
-            nc.vector.tensor_copy(windows[min(m, 2)][:].indirect(offsets[:]), gv[:, m, :])
-
-        def add_and_store(m, backs):
             res = sb.tile([P, T], F32, name="res%d" % m)
-            pieces = (0, 512, 768, 1024) if m == E // P - 1 else (0, 512, 1024)
             for lo, hi in zip(pieces, pieces[1:]):
-                cols = slice(lo, hi)
                 nc.vector.tensor_tensor(
-                    res[:, cols], backs[lo // BANK][:, lo % BANK : lo % BANK + hi - lo], windows[min(m, 2)][:, cols], ALU.add
+                    res[:, lo:hi], backs[lo // BANK][:, lo % BANK : lo % BANK + hi - lo], windows[m][:, lo:hi], ALU.add
                 )
-                if m == E // P - 1:
-                    nc.sync.dma_start(out=out[m * P : (m + 1) * P, cols], in_=res[:, cols])
-            if m < E // P - 1:
-                nc.sync.dma_start(out=out[m * P : (m + 1) * P, :], in_=res[:])
+                nc.sync.dma_start(out=out[m * P : (m + 1) * P, lo:hi], in_=res[:, lo:hi])
 
-        for h in range(2):
-            nc.vector.tensor_copy(windows[0][:].indirect(offsets[:, 8 * h : 8 * h + 8]), gv[:, 0, h * P : (h + 1) * P])
-        scatter(1)
-        scatter(2)
-        late = []
-        for m in range(2):
+        for m, pieces in ((0, (0, 1024)), (1, (0, 512, 1024))):
             faded = sb.tile([P, T], F32, name="faded%d" % m, tag=("faded0", "s_then_g_bf_then_faded")[m], align_bytes=64)
             nc.gpsimd.tensor_tensor(faded[:], old_sb[m][:], fade_all[:], ALU.mult)
             res = sb.tile([P, T], F32, name="res%d" % m)
-            if m == 0:
-                nc.gpsimd.tensor_tensor(res[:], faded[:], windows[m][:], ALU.add)
-                nc.sync.dma_start(out=out[m * P : (m + 1) * P, :], in_=res[:])
-            else:
-                for h in range(2):
-                    cols = slice(h * BANK, (h + 1) * BANK)
-                    nc.gpsimd.tensor_tensor(res[:, cols], faded[:, cols], windows[m][:, cols], ALU.add)
-                    late.append((out[m * P : (m + 1) * P, cols], res[:, cols]))
-        add_and_store(2, faded_old_in_psum(2, (2, 3), (6, 7)))
-        scatter(3)
-        add_and_store(3, faded_old_in_psum(3, (4, 5), (0, 1)))
-        for dst, src in late:
-            nc.scalar.dma_start(out=dst, in_=src)
+            for lo, hi in zip(pieces, pieces[1:]):
+                nc.gpsimd.tensor_tensor(res[:, lo:hi], faded[:, lo:hi], windows[m][:, lo:hi], ALU.add)
+                nc.scalar.dma_start(out=out[m * P : (m + 1) * P, lo:hi], in_=res[:, lo:hi])

from contextlib import ExitStack

import concourse.mybir as mybir
from concourse.masks import make_identity

D, E, T, I, Q, G = 512, 512, 1024, 256, 512, 32
FLOPS = 2 * D * Q * I + 2 * Q * E * I

F32 = mybir.dt.float32
BF16 = mybir.dt.bfloat16
I32 = mybir.dt.int32
U32 = mybir.dt.uint32
U16 = mybir.dt.uint16
U8 = mybir.dt.uint8
FP8X4 = mybir.dt.float8_e4m3fn_x4
ALU = mybir.AluOpType
ACT = mybir.ActivationFunctionType
AX = mybir.AxisListType

P = 128
PACK = 4
BANK = 512
GROUP = I // G


def tile_attend_bmixednorm_v_kernel(tc, query, keys_words, keys_scales, share, qs, grows, old, fade, offs, out):
    nc = tc.nc
    with ExitStack() as ctx:
        sb = ctx.enter_context(tc.tile_pool(name="sb", bufs=1))
        ps = ctx.enter_context(tc.psum_pool(name="ps", bufs=1))

        def bank(n, name):
            return ps.tile([P, BANK], F32, name=name, tag="bank%d" % n)

        offsets = sb.tile([P, I // 16], U16, name="offsets")
        key_bytes = sb.tile([P, T], U8, name="key_bytes", align_bytes=64)
        nc.gpsimd.memset(key_bytes[:].bitcast(I32), 0)
        nc.sync.dma_start(offsets[:], offs)
        fade_runs = sb.tile([P, T // P], F32, name="fade_runs", tag="fade_runs_then_q_bytes", align_bytes=64)
        nc.sync.dma_start(out=fade_runs[:], in_=fade.rearrange("o (p j) -> (o p) j", p=P))
        query_rows = query.rearrange("(p j) q -> p j q", j=PACK)
        q_raw = [sb.tile([P, PACK, Q // 2], F32, name="q_raw%d" % h) for h in range(2)]
        nc.sync.dma_start(out=q_raw[0][:], in_=query_rows[:, :, 0 : Q // 2])
        for quad in range(4):
            nc.sync.dma_start(
                out=key_bytes[32 * quad : 32 * quad + 4, :].bitcast(I32),
                in_=keys_scales[0, 4 * quad : 4 * quad + 4, :].bitcast(I32),
            )
        nc.sync.dma_start(out=q_raw[1][:], in_=query_rows[:, :, Q // 2 : Q])
        key_words = sb.tile([P, T], U32, name="key_words", align_bytes=64)
        nc.sync.dma_start(out=key_words[:].bitcast(I32), in_=keys_words[0].rearrange("p n t -> p (n t)").bitcast(I32))
        share_sb = sb.tile([P, PACK], F32, name="share_sb")
        nc.sync.dma_start(out=share_sb[:], in_=share.rearrange("(p r) o -> p (r o)", r=PACK))
        qs_sb = sb.tile([P, PACK], F32, name="qs_sb")
        nc.sync.dma_start(out=qs_sb[:], in_=qs.rearrange("(p r) o -> p (r o)", r=PACK))
        old_sb = [sb.tile([P, T], F32, name="old%d" % m) for m in range(E // P)]
        nc.sync.dma_start(out=old_sb[0][:], in_=old[0:P, :])
        g_raw = sb.tile([P, PACK, E], F32, name="g_raw")
        nc.sync.dma_start(out=g_raw[:], in_=grows.rearrange("(p r) e -> p r e", r=PACK))
        for m in range(1, E // P):
            nc.sync.dma_start(out=old_sb[m][:], in_=old[m * P : (m + 1) * P, :])

        ident = sb.tile([P, P], F32, name="ident")
        make_identity(nc, ident[:])
        windows = []
        for m in range(E // P):
            w = sb.tile([P, T], F32, name="window%d" % m)
            (nc.vector if m < 3 else nc.gpsimd).memset(w[:], 0.0)
            windows.append(w)

        fade_all = sb.tile([P, T], F32, name="fade_all")
        for h in range(2):
            spread = bank(h, "spread%d" % h)
            for k in range(4):
                j = 4 * h + k
                nc.tensor.transpose(spread[:, k * P : (k + 1) * P], fade_runs[:, j : j + 1].to_broadcast([P, P]), ident[:])
            nc.scalar.activation(
                fade_all[:].rearrange("p (n j) -> p n j", j=T // P)[:, :, 4 * h : 4 * h + 4],
                spread[:].rearrange("p (k n) -> p n k", n=P),
                ACT.Copy,
            )

        kg_bytes = sb.tile([P, I], U8, name="kg_bytes", align_bytes=64)
        nc.vector.tensor_copy(kg_bytes[:], key_bytes[:].indirect(offsets[:]))

        q_bf = sb.tile([P, PACK, P, PACK], BF16, name="q_bf", align_bytes=64)
        for h in range(2):
            nc.vector.tensor_copy(
                out=q_bf[:, :, h * (P // 2) : (h + 1) * (P // 2), :].rearrange("p r s j -> p s j r"),
                in_=q_raw[h][:].rearrange("p j (s r) -> p s j r", r=PACK),
            )
        q_words = sb.tile([P, Q], U32, name="q_words", align_bytes=64)
        q_bytes = sb.tile([P, Q], U8, name="q_bytes", tag="fade_runs_then_q_bytes", align_bytes=64)
        neg_max = sb.tile([P, PACK], F32, name="neg_max")
        p_sb = sb.tile([P, PACK, I], F32, name="p_sb")
        z_mix = sb.tile([P, PACK], F32, name="z_mix")
        nc.vector.quantize_mx(
            out=q_words[:].bitcast(FP8X4), scales=q_bytes[:], in_=q_bf[:].rearrange("p r s j -> p (r s j)")
        )
        kg_words = sb.tile([P, I], U32, name="kg_words", align_bytes=64)
        nc.vector.tensor_copy(kg_words[:], key_words[:].indirect(offsets[:]))
        scores = []
        for r in range(PACK):
            cols = slice(r * P, (r + 1) * P)
            a = bank(r, "scores%d" % r)
            nc.tensor.matmul_mx(
                out=a[:, 0:I],
                lhsT=q_words[:, cols].bitcast(FP8X4),
                lhsT_scale=q_bytes[:, cols],
                rhs=kg_words[:].bitcast(FP8X4),
                rhs_scale=kg_bytes[:],
                start=True,
                stop=True,
            )
            scores.append(a)

        inv_qs = sb.tile([P, PACK], F32, name="inv_qs")
        nc.vector.reciprocal(inv_qs[:], qs_sb[:])
        row_mix = sb.tile([P, PACK], F32, name="row_mix")
        nc.gpsimd.tensor_tensor(row_mix[:], share_sb[:], inv_qs[:], ALU.mult)
        rest = sb.tile([P, PACK], F32, name="rest")
        nc.gpsimd.tensor_scalar(rest[:], share_sb[:], -64.0, 64.0, ALU.mult, ALU.add)
        group_mix = sb.tile([P, PACK], F32, name="group_mix")
        nc.gpsimd.tensor_tensor(group_mix[:], rest[:], inv_qs[:], ALU.mult)

        for r in range(PACK):
            nc.vector.tensor_reduce(neg_max[:, r : r + 1], scores[r][:, 0:I], AX.X, ALU.max, negate=True)
            nc.scalar.activation(p_sb[:, r, :], scores[r][:, 0:I], ACT.Exp, bias=neg_max[:, r : r + 1])
        s = sb.tile([P, PACK, G], F32, name="s", tag="s_then_g_bf_then_faded", align_bytes=64)
        den = sb.tile([P, PACK, G], F32, name="den")
        v = sb.tile([P, G, PACK], F32, name="v")
        for r in range(PACK):
            nc.vector.tensor_reduce(s[:, r, :], p_sb[:, r, :].rearrange("p (g j) -> p g j", j=GROUP), AX.X, ALU.add)
            nc.scalar.activation(
                den[:, r, :], s[:, r, :], ACT.Copy, scale=row_mix[:, r : r + 1], accum_out=z_mix[:, r : r + 1]
            )
            nc.scalar.activation(
                den[:, r, :], s[:, r, :], ACT.Identity, bias=z_mix[:, r : r + 1], scale=group_mix[:, r : r + 1]
            )
        for r in range(PACK):
            nc.vector.reciprocal(v[:, :, r], den[:, r, :])

        g_bf = sb.tile([P, E, PACK], BF16, name="g_bf", tag="s_then_g_bf_then_faded", align_bytes=64)
        for m in range(E // P):
            cols = slice(m * P, (m + 1) * P)
            nc.scalar.copy(
                out=g_bf[:, cols, :].rearrange("p (c i) r -> p c r i", i=4),
                in_=g_raw[:, :, cols].rearrange("p r (c i) -> p c r i", i=4),
            )

        w_words = sb.tile([P, I], U32, name="w_words", align_bytes=64)
        w_bytes = sb.tile([P, I], U8, name="w_bytes", align_bytes=64)
        gv = sb.tile([P, E // P, I], F32, name="gv")
        g_bytes = sb.tile([P, E], U8, name="g_bytes", align_bytes=64)

        def quantize_grows(words, first, count):
            nc.vector.quantize_mx(
                out=words.bitcast(FP8X4),
                scales=g_bytes[:, first : first + count],
                in_=g_bf[:, first : first + count, :].rearrange("p e r -> p (e r)"),
            )

        g_first = sb.tile([P, P], U32, name="g_first", align_bytes=64)
        quantize_grows(g_first[:], 0, P)
        for h in range(2):
            gs = slice(h * (G // 2), (h + 1) * (G // 2))
            slots = slice(h * P, (h + 1) * P)
            w_bf = sb.tile([P, P, PACK], BF16, name="w_bf%d" % h, tag="w_bf%d" % h, align_bytes=64)
            for k in range(2):
                run = slice(4 * k, 4 * k + 4)
                nc.vector.tensor_tensor(
                    w_bf[:].rearrange("p (g j) r -> p g r j", j=GROUP)[:, :, :, run],
                    p_sb[:, :, slots].rearrange("p r (g j) -> p g r j", j=GROUP)[:, :, :, run],
                    v[:, gs, :].unsqueeze(3).to_broadcast([P, G // 2, PACK, 4]),
                    ALU.mult,
                )
            nc.vector.quantize_mx(
                out=w_words[:, slots].bitcast(FP8X4),
                scales=w_bytes[:, slots],
                in_=w_bf[:].rearrange("p i r -> p (i r)"),
            )
            first = bank(2 + h, "gv_first%d" % h)
            nc.tensor.matmul_mx(
                out=first[:, 0:P],
                lhsT=g_first[:].bitcast(FP8X4),
                lhsT_scale=g_bytes[:, 0:P],
                rhs=w_words[:, slots].bitcast(FP8X4),
                rhs_scale=w_bytes[:, slots],
                start=True,
                stop=True,
            )
            nc.scalar.copy(out=gv[:, 0, slots], in_=first[:, 0:P])
        g_rest = sb.tile([P, E - P], U32, name="g_rest", tag="w_bf1", align_bytes=64)
        quantize_grows(g_rest[:, 0:P], P, P)
        quantize_grows(g_rest[:, P : 3 * P], 2 * P, 2 * P)
        for m in range(1, E // P):
            if m != 3:
                others = bank(3 + m, "gv_others%d" % m)
            at = slice(I, 2 * I) if m == 3 else slice(0, I)
            nc.tensor.matmul_mx(
                out=others[:, at],
                lhsT=g_rest[:, (m - 1) * P : m * P].bitcast(FP8X4),
                lhsT_scale=g_bytes[:, m * P : (m + 1) * P],
                rhs=w_words[:].bitcast(FP8X4),
                rhs_scale=w_bytes[:],
                start=True,
                stop=True,
            )
            if m == 1:
                nc.scalar.copy(out=gv[:, 1, :], in_=others[:, 0:I])
        nc.scalar.copy(out=gv[:, 2:4, :], in_=others[:].rearrange("p (m i) -> p m i", i=I))

        fade_cols = sb.tile([P, T // P], F32, name="fade_cols")
        for h in range(2):
            turned_fade = bank(6 + h, "turned_fade%d" % h)
            for k in range(4):
                b = 4 * h + k
                nc.tensor.transpose(turned_fade[:, k * P : (k + 1) * P], fade_all[:, b * P : (b + 1) * P], ident[:])
            nc.scalar.activation(fade_cols[:, 4 * h : 4 * h + 4], turned_fade[:, 0:BANK:P], ACT.Copy)

        for h in range(2):
            nc.vector.tensor_copy(windows[0][:].indirect(offsets[:, 8 * h : 8 * h + 8]), gv[:, 0, h * P : (h + 1) * P])
        for m in range(1, E // P):
            nc.vector.tensor_copy(windows[m][:].indirect(offsets[:]), gv[:, m, :])

        faded_t = {}
        for m, banks in ((2, (2, 3)), (3, (4, 5))):
            faded_t[m] = sb.tile([P, T // P, P], F32, name="faded_t%d" % m)
            for h in range(2):
                turned = bank(banks[h], "turned%d_%d" % (m, h))
                for k in range(4):
                    b = 4 * h + k
                    nc.tensor.transpose(turned[:, k * P : (k + 1) * P], old_sb[m][:, b * P : (b + 1) * P], ident[:])
                for k in range(4):
                    b = 4 * h + k
                    nc.scalar.activation(
                        faded_t[m][:, b, :], turned[:, k * P : (k + 1) * P], ACT.Copy, scale=fade_cols[:, b : b + 1]
                    )
        for m, banks, pieces in ((2, (6, 7), (0, 512, 1024)), (3, (0, 1), (0, 512, 768, 1024))):
            backs = []
            for h in range(2):
                back = bank(banks[h], "back%d_%d" % (m, h))
                for k in range(4):
                    nc.tensor.transpose(back[:, k * P : (k + 1) * P], faded_t[m][:, 4 * h + k, :], ident[:])
                backs.append(back)
            res = sb.tile([P, T], F32, name="res%d" % m)
            for lo, hi in zip(pieces, pieces[1:]):
                nc.vector.tensor_tensor(
                    res[:, lo:hi], backs[lo // BANK][:, lo % BANK : lo % BANK + hi - lo], windows[m][:, lo:hi], ALU.add
                )
                nc.sync.dma_start(out=out[m * P : (m + 1) * P, lo:hi], in_=res[:, lo:hi])

        for m, pieces in ((0, (0, 1024)), (1, (0, 512, 1024))):
            faded = sb.tile([P, T], F32, name="faded%d" % m, tag=("faded0", "s_then_g_bf_then_faded")[m], align_bytes=64)
            nc.gpsimd.tensor_tensor(faded[:], old_sb[m][:], fade_all[:], ALU.mult)
            res = sb.tile([P, T], F32, name="res%d" % m)
            for lo, hi in zip(pieces, pieces[1:]):
                nc.gpsimd.tensor_tensor(res[:, lo:hi], faded[:, lo:hi], windows[m][:, lo:hi], ALU.add)
                nc.scalar.dma_start(out=out[m * P : (m + 1) * P, lo:hi], in_=res[:, lo:hi])
